import numpy as np
import ml_dtypes


def mxq(x, axis, fmt="e4m3"):
    dtype, down = {"e4m3": (ml_dtypes.float8_e4m3fn, 7), "e5m2": (ml_dtypes.float8_e5m2, 14)}[fmt]
    v = np.moveaxis(np.asarray(x, np.float32).astype(ml_dtypes.bfloat16).astype(np.float64), axis, -1)
    blocks = v.reshape(v.shape[:-1] + (-1, 32))
    amax = np.abs(blocks).max(-1, keepdims=True)
    byte = np.maximum(np.where(amax > 0, np.frexp(amax)[1] - 1 + 127, 0) - down, 1)
    scale = np.exp2(byte - 127.0)
    codes = (blocks / scale).astype(np.float32).astype(dtype).astype(np.float64)
    return np.moveaxis((codes * scale).reshape(v.shape), -1, axis)


WIDE = False


def mx_kscale(k):
    if not WIDE:
        return np.ones(k)
    levels = np.array([10, -10, 5, -5, 0])
    if k % 512:
        return np.exp2(np.random.permutation(np.resize(levels, k // 32))).repeat(32)
    a = np.empty((k // 512, 16))
    for p in range(k // 512):
        a[p, :8] = np.random.permutation(np.resize(levels, 8))
        for g in range(8):
            far = levels[np.abs(levels - a[p, g]) >= 10]
            a[p, g + 8] = far[np.random.randint(len(far))]
    return np.exp2(a.ravel()).repeat(32)


def f64(x):
    return np.asarray(x).astype(np.float64)


def striped(idx):
    return np.tile(np.asarray(idx).reshape(-1, 16).T, (8, 1)).astype(np.uint16)


def unstriped(offs):
    return offs[:16].T.reshape(-1).astype(np.int64)


E2M1 = np.array([0.0, 0.5, 1.0, 1.5, 2.0, 3.0, 4.0, 6.0, -0.0, -0.5, -1.0, -1.5, -2.0, -3.0, -4.0, -6.0])


def pack_weight(w, fmt):
    k, n = w.shape
    w = f64(np.asarray(w, np.float32).astype(ml_dtypes.bfloat16)).reshape(k // 32, 32, n)
    amax = np.abs(w).max(1)
    if fmt == "e4m3":
        byte = np.frexp(amax)[1] - 1 + 127 - 7
    else:
        mant, ex = np.frexp(amax / 6.0)
        byte = np.where(mant > 0.5, ex, ex - 1) + 127
    byte = np.clip(np.where(amax > 0, byte, 1), 1, 254)
    scaled = (w * np.exp2(127.0 - byte)[:, None, :]).reshape(k, n).astype(np.float32)
    by_word = np.ascontiguousarray(scaled.reshape(k // 512, 128, 4, n).transpose(0, 1, 3, 2))
    if fmt == "e4m3":
        words = by_word.astype(ml_dtypes.float8_e4m3fn).view(np.uint8)
    else:
        c = by_word.astype(ml_dtypes.float4_e2m1fn).view(np.uint8) & 0xF
        words = (c[..., 0::2] | (c[..., 1::2] << 4)).reshape(k // 512, 128, 2 * n)
    return np.ascontiguousarray(words), np.ascontiguousarray(byte.astype(np.uint8).reshape(k // 512, 16, n))


def unpack_weight(words, scales, fmt):
    g, _, n = scales.shape
    words = np.ascontiguousarray(words).reshape(g, 128, n, -1)
    if fmt == "e4m3":
        vals = words.view(ml_dtypes.float8_e4m3fn).astype(np.float64)
    else:
        nib = np.empty((g, 128, n, 4), np.uint8)
        nib[..., 0::2] = words & 0xF
        nib[..., 1::2] = words >> 4
        vals = E2M1[nib]
    vals = vals * np.repeat(np.exp2(scales.astype(np.float64) - 127.0), 8, axis=1)[..., None]
    return vals.transpose(0, 1, 3, 2).reshape(g * 512, n)


D, E, T, I, Q = 512, 512, 1024, 256, 512


def setup_inputs():
    n = np.random.standard_normal
    idx = np.random.permutation(T)[:I]
    fd = mx_kscale(D)
    fq = mx_kscale(Q)
    keysp = pack_weight(n((D, T)) / fd[:, None], "e2m1")
    return {
        "query": (n((D, Q)) * 0.5 / np.sqrt(D) * fd[:, None]).astype(np.float32),
        "qs": (np.random.uniform(8.0, 32.0, (Q, 1)) * fq[:, None]).astype(np.float32),
        "grows": (n((Q, E)) / fq[:, None]).astype(np.float32),
        "vals": (n((E, T))).astype(np.float32),
        "keys_words": keysp[0],
        "keys_scales": keysp[1],
        "gain": (np.random.uniform(0.5, 2.0, (E, 1))).astype(np.float32),
        "sg": (np.random.uniform(0.5, 2.0, (1, I))).astype(np.float32),
        "old": (n((E, T)) * 1.0).astype(np.float32),
        "fade": (np.random.uniform(0.5, 1.0, (1, T))).astype(np.float32),
        "offs": striped(idx),
    }


def reference(query, qs, grows, vals, keys_words, keys_scales, gain, sg, old, fade, offs):
    idx = unstriped(offs)
    keysu = unpack_weight(keys_words, keys_scales, "e2m1")
    queryq = mxq(f64(query), 0, "e4m3")
    keysidxg = keysu[:, idx]
    a = queryq.T @ keysidxg
    p = np.exp(a - np.max(a, axis=1, keepdims=True))
    w = p * f64(qs) / np.sum(p, axis=1, keepdims=True)
    growsq = mxq(f64(grows), 0, "e4m3")
    wq = mxq(w, 0, "e4m3")
    c0 = growsq.T @ wq
    x1 = f64(vals)[:, idx] * f64(gain)
    vp = np.tanh(x1)
    dx1 = c0 * (1.0 - np.square(vp))
    gs = dx1 * f64(sg)
    gf = np.zeros((E, T))
    gf[:, idx] = gs
    y = f64(old) * f64(fade) + gf
    return y

@@ -1,0 +1,256 @@
+from contextlib import ExitStack
+
+import concourse.mybir as mybir
+from concourse.masks import make_identity
+
+D, E, T, I, Q = 512, 512, 1024, 256, 512
+FLOPS = 2 * D * Q * I + 2 * Q * E * I
+
+F32 = mybir.dt.float32
+BF16 = mybir.dt.bfloat16
+I32 = mybir.dt.int32
+U32 = mybir.dt.uint32
+U16 = mybir.dt.uint16
+U8 = mybir.dt.uint8
+FP8X4 = mybir.dt.float8_e4m3fn_x4
+FP4X4 = mybir.dt.float4_e2m1fn_x4
+ALU = mybir.AluOpType
+ACT = mybir.ActivationFunctionType
+AX = mybir.AxisListType
+
+P = 128
+PACK = 4
+TILES = E // P
+BLOCKS = T // P
+BANK = 512
+
+
+def tile_attend_bvtanh_s_kernel(tc, query, qs, grows, vals, keys_words, keys_scales, gain, sg, old, fade, offs, out):
+    nc = tc.nc
+    with ExitStack() as ctx:
+        keep = ctx.enter_context(tc.tile_pool(name="keep", bufs=1))
+        psum = ctx.enter_context(tc.psum_pool(name="psum", bufs=1))
+
+        def sb(name, shape, dtype):
+            return keep.tile(shape, dtype, name=name, align_bytes=64)
+
+        def bank(b, name):
+            return psum.tile([P, BANK], F32, name=name, tag="bank%d" % b)
+
+        key_planes = sb("key_planes", [P, T], U8)
+        nc.vector.memset(key_planes[:].bitcast(I32), 0)
+        rows = sb("rows", [P, P], F32)
+        nc.vector.memset(rows[:], 0.0)
+        ident = sb("ident", [P, P], F32)
+        make_identity(nc, ident[:])
+        warm = sb("warm", [P, 8], F32)
+        nc.vector.memset(warm[:], 0.0)
+        warm_out = sb("warm_out", [P, 8], F32)
+        nc.scalar.activation(warm_out[:], warm[:], ACT.Exp)
+
+        offsets = sb("offsets", [P, I // 16], U16)
+        nc.sync.dma_start(offsets[:], offs)
+        key_words = sb("key_words", [P, T], U16)
+        nc.sync.dma_start(key_words[:].bitcast(I32), keys_words[0].bitcast(I32))
+        for quad in range(4):
+            nc.scalar.dma_start(
+                key_planes[32 * quad : 32 * quad + 4, :].bitcast(I32),
+                keys_scales[0, 4 * quad : 4 * quad + 4, :].bitcast(I32),
+            )
+        query_rows = query.rearrange("(p j) q -> p j q", j=PACK)
+        grows_rows = grows.rearrange("(p j) e -> p j e", j=PACK)
+        q_raw = [sb("q_raw%d" % h, [P, PACK, Q // 2], F32) for h in range(2)]
+        g_raw = [sb("g_raw%d" % h, [P, PACK, E // 2], F32) for h in range(2)]
+        for h in range(2):
+            nc.sync.dma_start(q_raw[h][:], query_rows[:, :, h * 256 : (h + 1) * 256])
+        qs_cols = sb("qs_cols", [P, PACK], F32)
+        val_pool = [sb("val_pool%d" % k, [P, T], F32) for k in range(TILES)]
+        old_pair = [sb("old_pair%d" % a, [P, 2, T], F32) for a in range(2)]
+        old_rows = old.rearrange("(k p) t -> p k t", p=P)
+
+        def load_vals(k):
+            nc.sync.dma_start(val_pool[k][:], vals[k * P : (k + 1) * P, :])
+
+        nc.sync.dma_start(g_raw[0][:], grows_rows[:, :, 0:256])
+        load_vals(0)
+        nc.sync.dma_start(qs_cols[:], qs.rearrange("(p r) o -> p (r o)", r=PACK))
+        nc.sync.dma_start(rows[8:12, :], gain.rearrange("(k n) o -> k (n o)", n=P))
+        load_vals(1)
+        nc.sync.dma_start(rows[12:14, :], sg.rearrange("o (c n) -> (o c) n", n=P))
+        nc.sync.dma_start(rows[0:8, :], fade.rearrange("o (c n) -> (o c) n", n=P))
+        nc.sync.dma_start(old_pair[0][:], old_rows[:, 0:2, :])
+        nc.sync.dma_start(g_raw[1][:], grows_rows[:, :, 256:512])
+        load_vals(2)
+        load_vals(3)
+        nc.sync.dma_start(old_pair[1][:], old_rows[:, 2:4, :])
+
+        windows = [sb("window%d" % k, [P, T], F32) for k in range(3)]
+        nc.vector.memset(windows[0][:], 0.0)
+        for k in range(1, 3):
+            nc.gpsimd.memset(windows[k][:], 0.0)
+        windows.append(windows[0])
+
+        keys_g = sb("keys_g", [P, I], U16)
+        nc.vector.tensor_copy(keys_g[:], key_words[:].indirect(offsets[:]))
+        planes_g = sb("planes_g", [P, I], U8)
+        nc.vector.tensor_copy(planes_g[:], key_planes[:].indirect(offsets[:]))
+
+        q_bf = sb("q_bf", [P, PACK, P, PACK], BF16)
+        for h in range(2):
+            nc.vector.tensor_copy(
+                q_bf[:, :, 64 * h : 64 * h + 64, :].rearrange("p r s j -> p s j r"),
+                q_raw[h][:].rearrange("p j (s r) -> p s j r", r=PACK),
+            )
+        q_codes = sb("q_codes", [P, Q], U32)
+        q_planes = sb("q_planes", [P, Q], U8)
+        for h in range(2):
+            nc.vector.quantize_mx(
+                out=q_codes[:, 256 * h : 256 * h + 256].bitcast(FP8X4),
+                scales=q_planes[:, 256 * h : 256 * h + 256],
+                in_=q_bf[:, 2 * h : 2 * h + 2, :, :].rearrange("p r s j -> p (r s j)"),
+            )
+
+        g_bf = [sb("g_bf%d" % h, [P, E // 2, PACK], BF16) for h in range(2)]
+        g_codes = sb("g_codes", [P, E], U32)
+        g_planes = sb("g_planes", [P, E], U8)
+
+        def cast_grows(h):
+            nc.scalar.copy(
+                g_bf[h][:].rearrange("p (c i) j -> p c j i", i=4),
+                g_raw[h][:].rearrange("p j (c i) -> p c j i", i=4),
+            )
+
+        def quantise_grows(h):
+            nc.vector.quantize_mx(
+                out=g_codes[:, 256 * h : 256 * h + 256].bitcast(FP8X4),
+                scales=g_planes[:, 256 * h : 256 * h + 256],
+                in_=g_bf[h][:].rearrange("p e j -> p (e j)"),
+            )
+
+        cast_grows(0)
+
+        neg_max = sb("neg_max", [P, PACK], F32)
+        sums = sb("sums", [P, PACK], F32)
+        probs = sb("probs", [P, PACK, I], F32)
+        for r in range(PACK):
+            scores = bank(r, "scores%d" % r)
+            nc.tensor.matmul_mx(
+                out=scores[:, 0:I],
+                lhsT=q_codes[:, r * P : (r + 1) * P].bitcast(FP8X4),
+                lhsT_scale=q_planes[:, r * P : (r + 1) * P],
+                rhs=keys_g[:].bitcast(FP4X4),
+                rhs_scale=planes_g[:],
+                start=True,
+                stop=True,
+            )
+            nc.vector.tensor_reduce(neg_max[:, r : r + 1], scores[:, 0:I], AX.X, ALU.max, negate=True)
+            nc.scalar.activation(
+                probs[:, r, :], scores[:, 0:I], ACT.Exp, bias=neg_max[:, r : r + 1], accum_out=sums[:, r : r + 1]
+            )
+        turned = bank(4, "turned")
+        nc.tensor.transpose(turned[:, 0:P], rows[:], ident[:])
+        cols = sb("cols", [P, 16], F32)
+        nc.scalar.copy(cols[:], turned[:, 0:16])
+        spread = bank(5, "spread")
+        for c in range(2):
+            nc.tensor.transpose(spread[:, c * P : (c + 1) * P], cols[:, 12 + c : 13 + c].to_broadcast([P, P]), ident[:])
+        neg_sg = sb("neg_sg", [P, I], F32)
+        nc.scalar.activation(neg_sg[:], spread[:, 0:I], ACT.Copy, scale=-1.0)
+
+        quantise_grows(0)
+        inv = sb("inv", [P, PACK], F32)
+        nc.vector.reciprocal(inv[:], sums[:])
+        factor = sb("factor", [P, PACK], F32)
+        nc.vector.tensor_tensor(factor[:], inv[:], qs_cols[:], ALU.mult)
+        w_bf = sb("w_bf", [P, I, PACK], BF16)
+        nc.vector.tensor_tensor(
+            w_bf[:].rearrange("p (c i) r -> p c r i", i=4),
+            probs[:].rearrange("p r (c i) -> p c r i", i=4),
+            factor[:].unsqueeze(1).unsqueeze(3).to_broadcast([P, I // 4, PACK, 4]),
+            ALU.mult,
+        )
+        w_codes = sb("w_codes", [P, I], U32)
+        w_planes = sb("w_planes", [P, I], U8)
+        nc.vector.quantize_mx(out=w_codes[:].bitcast(FP8X4), scales=w_planes[:], in_=w_bf[:].rearrange("p i r -> p (i r)"))
+
+        c0 = [bank(6 + a, "c0_%d" % a) for a in range(2)]
+
+        def product(k):
+            nc.tensor.matmul_mx(
+                out=c0[k // 2][:, (k % 2) * I : (k % 2 + 1) * I],
+                lhsT=g_codes[:, k * P : (k + 1) * P].bitcast(FP8X4),
+                lhsT_scale=g_planes[:, k * P : (k + 1) * P],
+                rhs=w_codes[:].bitcast(FP8X4),
+                rhs_scale=w_planes[:],
+                start=True,
+                stop=True,
+            )
+
+        picked = [sb("picked%d" % k, [P, I], F32) for k in range(TILES)]
+        vp = [sb("vp%d" % k, [P, I], F32) for k in range(TILES)]
+        vp2 = [sb("vp2_%d" % k, [P, I], F32) for k in range(TILES)]
+        neg_dx = [sb("neg_dx%d" % k, [P, I], F32) for k in range(TILES)]
+
+        def prepare(k):
+            nc.vector.tensor_copy(picked[k][:], val_pool[k][:].indirect(offsets[:]))
+            nc.scalar.activation(vp[k][:], picked[k][:], ACT.Tanh, scale=cols[:, 8 + k : 9 + k])
+            nc.scalar.activation(vp2[k][:], vp[k][:], ACT.Square)
+
+        def scatter(k):
+            nc.vector.scalar_tensor_tensor(
+                neg_dx[k][:], vp2[k][:], 1.0, c0[k // 2][:, (k % 2) * I : (k % 2 + 1) * I], ALU.subtract, ALU.mult
+            )
+            nc.vector.tensor_tensor(windows[k][:].indirect(offsets[:]), neg_dx[k][:], neg_sg[:], ALU.mult)
+
+        faded_t = [sb("faded_t%d" % a, [P, BLOCKS, 2 * P], F32) for a in range(2)]
+
+        def fade_pair(a):
+            for cc in range(BLOCKS // 2):
+                stage = bank(4 + cc % 2, "stage%d_%d" % (a, cc))
+                for c2 in range(2):
+                    c = 2 * cc + c2
+                    for k2 in range(2):
+                        nc.tensor.transpose(
+                            stage[:, (2 * c2 + k2) * P : (2 * c2 + k2 + 1) * P],
+                            old_pair[a][:, k2, c * P : (c + 1) * P],
+                            ident[:],
+                        )
+                for c2 in range(2):
+                    c = 2 * cc + c2
+                    nc.scalar.activation(
+                        faded_t[a][:, c, :], stage[:, 2 * c2 * P : 2 * (c2 + 1) * P], ACT.Copy, scale=cols[:, c : c + 1]
+                    )
+
+        def finish(k):
+            for h in range(2):
+                faded = bank(2 * (k % 2) + h, "faded%d_%d" % (k, h))
+                for c4 in range(4):
+                    nc.tensor.transpose(
+                        faded[:, c4 * P : (c4 + 1) * P],
+                        faded_t[k // 2][:, 4 * h + c4, (k % 2) * P : (k % 2 + 1) * P],
+                        ident[:],
+                    )
+                result = sb("result%d_%d" % (k, h), [P, BANK], F32)
+                nc.vector.tensor_tensor(result[:], faded[:], windows[k][:, h * BANK : (h + 1) * BANK], ALU.add)
+                nc.sync.dma_start(out[k * P : (k + 1) * P, h * BANK : (h + 1) * BANK], result[:])
+
+        prepare(0)
+        product(0)
+        product(1)
+        scatter(0)
+        prepare(1)
+        scatter(1)
+        fade_pair(0)
+        cast_grows(1)
+        quantise_grows(1)
+        product(2)
+        product(3)
+        prepare(2)
+        finish(0)
+        prepare(3)
+        scatter(2)
+        fade_pair(1)
+        finish(1)
+        scatter(3)
+        finish(2)
+        finish(3)

@@ -23,6 +23,7 @@ PACK = 4
 TILES = E // P
 BLOCKS = T // P
 BANK = 512
+LATE_TAGS = ("neg_slope0", "vp2_1")
 
 
 def tile_attend_bvtanh_s_kernel(tc, query, qs, grows, vals, keys_words, keys_scales, gain, sg, old, fade, offs, out):
@@ -31,8 +32,8 @@ def tile_attend_bvtanh_s_kernel(tc, query, qs, grows, vals, keys_words, keys_sca
         keep = ctx.enter_context(tc.tile_pool(name="keep", bufs=1))
         psum = ctx.enter_context(tc.psum_pool(name="psum", bufs=1))
 
-        def sb(name, shape, dtype):
-            return keep.tile(shape, dtype, name=name, align_bytes=64)
+        def sb(name, shape, dtype, tag=None):
+            return keep.tile(shape, dtype, name=name, tag=tag or name, align_bytes=64)
 
         def bank(b, name):
             return psum.tile([P, BANK], F32, name=name, tag="bank%d" % b)
@@ -43,46 +44,45 @@ def tile_attend_bvtanh_s_kernel(tc, query, qs, grows, vals, keys_words, keys_sca
         nc.vector.memset(rows[:], 0.0)
         ident = sb("ident", [P, P], F32)
         make_identity(nc, ident[:])
-        warm = sb("warm", [P, 8], F32)
-        nc.vector.memset(warm[:], 0.0)
-        warm_out = sb("warm_out", [P, 8], F32)
-        nc.scalar.activation(warm_out[:], warm[:], ACT.Exp)
 
         offsets = sb("offsets", [P, I // 16], U16)
         nc.sync.dma_start(offsets[:], offs)
         key_words = sb("key_words", [P, T], U16)
         nc.sync.dma_start(key_words[:].bitcast(I32), keys_words[0].bitcast(I32))
         for quad in range(4):
-            nc.scalar.dma_start(
+            (nc.scalar if quad < 2 else nc.sync).dma_start(
                 key_planes[32 * quad : 32 * quad + 4, :].bitcast(I32),
                 keys_scales[0, 4 * quad : 4 * quad + 4, :].bitcast(I32),
             )
+        qs_cols = sb("qs_cols", [P, PACK], F32)
+        warm_out = sb("warm_out", [P, 8], F32)
+        nc.scalar.activation(warm_out[:], ident[:, 0:8], ACT.Exp)
         query_rows = query.rearrange("(p j) q -> p j q", j=PACK)
         grows_rows = grows.rearrange("(p j) e -> p j e", j=PACK)
         q_raw = [sb("q_raw%d" % h, [P, PACK, Q // 2], F32) for h in range(2)]
         g_raw = [sb("g_raw%d" % h, [P, PACK, E // 2], F32) for h in range(2)]
-        for h in range(2):
-            nc.sync.dma_start(q_raw[h][:], query_rows[:, :, h * 256 : (h + 1) * 256])
-        qs_cols = sb("qs_cols", [P, PACK], F32)
         val_pool = [sb("val_pool%d" % k, [P, T], F32) for k in range(TILES)]
-        old_pair = [sb("old_pair%d" % a, [P, 2, T], F32) for a in range(2)]
-        old_rows = old.rearrange("(k p) t -> p k t", p=P)
+        old_tile = {k: sb("old_tile%d" % k, [P, T], F32) for k in (0, 2)}
 
         def load_vals(k):
             nc.sync.dma_start(val_pool[k][:], vals[k * P : (k + 1) * P, :])
 
+        for h in range(2):
+            nc.sync.dma_start(q_raw[h][:], query_rows[:, :, h * 256 : (h + 1) * 256])
         nc.sync.dma_start(g_raw[0][:], grows_rows[:, :, 0:256])
-        load_vals(0)
-        nc.sync.dma_start(qs_cols[:], qs.rearrange("(p r) o -> p (r o)", r=PACK))
-        nc.sync.dma_start(rows[8:12, :], gain.rearrange("(k n) o -> k (n o)", n=P))
-        load_vals(1)
-        nc.sync.dma_start(rows[12:14, :], sg.rearrange("o (c n) -> (o c) n", n=P))
         nc.sync.dma_start(rows[0:8, :], fade.rearrange("o (c n) -> (o c) n", n=P))
-        nc.sync.dma_start(old_pair[0][:], old_rows[:, 0:2, :])
+        nc.sync.dma_start(rows[8:12, :], gain.rearrange("(k n) o -> k (n o)", n=P))
+        nc.sync.dma_start(rows[12:14, :], sg.rearrange("o (c n) -> (o c) n", n=P))
+        nc.sync.dma_start(qs_cols[:], qs.rearrange("(p r) o -> p (r o)", r=PACK))
+        load_vals(0)
+        load_vals(1)
         nc.sync.dma_start(g_raw[1][:], grows_rows[:, :, 256:512])
         load_vals(2)
         load_vals(3)
-        nc.sync.dma_start(old_pair[1][:], old_rows[:, 2:4, :])
+        nc.sync.dma_start(old_tile[0][:], old[0 * P : 1 * P, :])
+        old_pair = sb("old_pair", [P, 2, T], F32)
+        nc.sync.dma_start(old_pair[:], old.rearrange("(a b p) t -> p a b t", p=P, b=2)[:, :, 1, :])
+        nc.sync.dma_start(old_tile[2][:], old[2 * P : 3 * P, :])
 
         windows = [sb("window%d" % k, [P, T], F32) for k in range(3)]
         nc.vector.memset(windows[0][:], 0.0)
@@ -96,34 +96,36 @@ def tile_attend_bvtanh_s_kernel(tc, query, qs, grows, vals, keys_words, keys_sca
         nc.vector.tensor_copy(planes_g[:], key_planes[:].indirect(offsets[:]))
 
         q_bf = sb("q_bf", [P, PACK, P, PACK], BF16)
-        for h in range(2):
-            nc.vector.tensor_copy(
-                q_bf[:, :, 64 * h : 64 * h + 64, :].rearrange("p r s j -> p s j r"),
-                q_raw[h][:].rearrange("p j (s r) -> p s j r", r=PACK),
+        for h, lo, hi, copy in ((0, 0, 64, nc.vector.tensor_copy), (1, 0, 40, nc.vector.tensor_copy), (1, 40, 64, nc.scalar.copy)):
+            copy(
+                q_bf[:, :, 64 * h + lo : 64 * h + hi, :].rearrange("p r s j -> p s r j"),
+                q_raw[h][:].rearrange("p j (s r) -> p s r j", r=PACK)[:, lo:hi],
             )
         q_codes = sb("q_codes", [P, Q], U32)
         q_planes = sb("q_planes", [P, Q], U8)
-        for h in range(2):
+        for lo, hi in ((0, 1), (1, 2), (2, 4)):
             nc.vector.quantize_mx(
-                out=q_codes[:, 256 * h : 256 * h + 256].bitcast(FP8X4),
-                scales=q_planes[:, 256 * h : 256 * h + 256],
-                in_=q_bf[:, 2 * h : 2 * h + 2, :, :].rearrange("p r s j -> p (r s j)"),
+                out=q_codes[:, P * lo : P * hi].bitcast(FP8X4),
+                scales=q_planes[:, P * lo : P * hi],
+                in_=q_bf[:, lo:hi, :, :].rearrange("p r s j -> p (r s j)"),
             )
 
-        g_bf = [sb("g_bf%d" % h, [P, E // 2, PACK], BF16) for h in range(2)]
-        g_codes = sb("g_codes", [P, E], U32)
-        g_planes = sb("g_planes", [P, E], U8)
+        g_bf = []
+        g_codes, g_planes = [], []
 
-        def cast_grows(h):
+        def cast_grows(h, tag=None):
+            g_bf.append(sb("g_bf%d" % h, [P, E // 2, PACK], BF16, tag))
             nc.scalar.copy(
                 g_bf[h][:].rearrange("p (c i) j -> p c j i", i=4),
                 g_raw[h][:].rearrange("p j (c i) -> p c j i", i=4),
             )
 
-        def quantise_grows(h):
+        def quantise_grows(h, tag=None):
+            g_codes.append(sb("g_codes%d" % h, [P, E // 2], U32, tag))
+            g_planes.append(sb("g_planes%d" % h, [P, E // 2], U8))
             nc.vector.quantize_mx(
-                out=g_codes[:, 256 * h : 256 * h + 256].bitcast(FP8X4),
-                scales=g_planes[:, 256 * h : 256 * h + 256],
+                out=g_codes[h][:].bitcast(FP8X4),
+                scales=g_planes[h][:],
                 in_=g_bf[h][:].rearrange("p e j -> p (e j)"),
             )
 
@@ -147,110 +149,161 @@ def tile_attend_bvtanh_s_kernel(tc, query, qs, grows, vals, keys_words, keys_sca
             nc.scalar.activation(
                 probs[:, r, :], scores[:, 0:I], ACT.Exp, bias=neg_max[:, r : r + 1], accum_out=sums[:, r : r + 1]
             )
+
         turned = bank(4, "turned")
         nc.tensor.transpose(turned[:, 0:P], rows[:], ident[:])
         cols = sb("cols", [P, 16], F32)
         nc.scalar.copy(cols[:], turned[:, 0:16])
-        spread = bank(5, "spread")
+        sg_rows = bank(5, "sg_rows")
         for c in range(2):
-            nc.tensor.transpose(spread[:, c * P : (c + 1) * P], cols[:, 12 + c : 13 + c].to_broadcast([P, P]), ident[:])
-        neg_sg = sb("neg_sg", [P, I], F32)
-        nc.scalar.activation(neg_sg[:], spread[:, 0:I], ACT.Copy, scale=-1.0)
+            nc.tensor.transpose(sg_rows[:, c * P : (c + 1) * P], cols[:, 12 + c : 13 + c].to_broadcast([P, P]), ident[:])
+
+        picked = []
+
+        def gather(k, tag=None):
+            picked.append(sb("picked%d" % k, [P, I], F32, tag))
+            nc.vector.tensor_copy(picked[k][:], val_pool[k][:].indirect(offsets[:]))
 
         quantise_grows(0)
-        inv = sb("inv", [P, PACK], F32)
+        gather(0)
+        inv = sb("inv", [P, PACK], F32, "val_pool0")
         nc.vector.reciprocal(inv[:], sums[:])
-        factor = sb("factor", [P, PACK], F32)
-        nc.vector.tensor_tensor(factor[:], inv[:], qs_cols[:], ALU.mult)
+        gather(1)
+        w_lin = sb("w_lin", [P, PACK, I], BF16, "val_pool1")
+        for r in range(PACK):
+            nc.vector.tensor_scalar(
+                w_lin[:, r, :], probs[:, r, :], inv[:, r : r + 1], qs_cols[:, r : r + 1], ALU.mult, ALU.mult
+            )
         w_bf = sb("w_bf", [P, I, PACK], BF16)
-        nc.vector.tensor_tensor(
-            w_bf[:].rearrange("p (c i) r -> p c r i", i=4),
-            probs[:].rearrange("p r (c i) -> p c r i", i=4),
-            factor[:].unsqueeze(1).unsqueeze(3).to_broadcast([P, I // 4, PACK, 4]),
-            ALU.mult,
+        nc.vector.tensor_copy(
+            w_bf[:].rearrange("p (c i) r -> p c r i", i=4), w_lin[:].rearrange("p r (c i) -> p c r i", i=4)
         )
+
+        neg_slope = []
+
+        def prepare(k, tag=None):
+            vp = sb("vp%d" % k, [P, I], F32, tag)
+            nc.scalar.activation(vp[:], picked[k][:], ACT.Tanh, scale=cols[:, 8 + k : 9 + k])
+            vp2 = sb("vp2_%d" % k, [P, I], F32)
+            nc.scalar.activation(vp2[:], vp[:], ACT.Square)
+            neg_slope.append(sb("neg_slope%d" % k, [P, I], F32))
+            nc.vector.scalar_tensor_tensor(neg_slope[k][:], vp2[:], 1.0, sg_rows[:, 0:I], ALU.subtract, ALU.mult)
+
+        prepare(0)
         w_codes = sb("w_codes", [P, I], U32)
         w_planes = sb("w_planes", [P, I], U8)
         nc.vector.quantize_mx(out=w_codes[:].bitcast(FP8X4), scales=w_planes[:], in_=w_bf[:].rearrange("p i r -> p (i r)"))
 
-        c0 = [bank(6 + a, "c0_%d" % a) for a in range(2)]
+        prepare(1)
+        fade_rows = sb("fade_rows", [P, T], F32, "vp1")
+        for h in range(2):
+            spread = bank(6 + h, "spread%d" % h)
+            for c4 in range(4):
+                c = 4 * h + c4
+                nc.tensor.transpose(spread[:, c4 * P : (c4 + 1) * P], cols[:, c : c + 1].to_broadcast([P, P]), ident[:])
+            nc.scalar.copy(fade_rows[:, h * BANK : (h + 1) * BANK], spread[:])
+
+        c0 = [bank(4, "c0_0"), bank(6, "c0_1")]
 
         def product(k):
             nc.tensor.matmul_mx(
                 out=c0[k // 2][:, (k % 2) * I : (k % 2 + 1) * I],
-                lhsT=g_codes[:, k * P : (k + 1) * P].bitcast(FP8X4),
-                lhsT_scale=g_planes[:, k * P : (k + 1) * P],
+                lhsT=g_codes[k // 2][:, (k % 2) * P : (k % 2 + 1) * P].bitcast(FP8X4),
+                lhsT_scale=g_planes[k // 2][:, (k % 2) * P : (k % 2 + 1) * P],
                 rhs=w_codes[:].bitcast(FP8X4),
                 rhs_scale=w_planes[:],
                 start=True,
                 stop=True,
             )
 
-        picked = [sb("picked%d" % k, [P, I], F32) for k in range(TILES)]
-        vp = [sb("vp%d" % k, [P, I], F32) for k in range(TILES)]
-        vp2 = [sb("vp2_%d" % k, [P, I], F32) for k in range(TILES)]
-        neg_dx = [sb("neg_dx%d" % k, [P, I], F32) for k in range(TILES)]
-
-        def prepare(k):
-            nc.vector.tensor_copy(picked[k][:], val_pool[k][:].indirect(offsets[:]))
-            nc.scalar.activation(vp[k][:], picked[k][:], ACT.Tanh, scale=cols[:, 8 + k : 9 + k])
-            nc.scalar.activation(vp2[k][:], vp[k][:], ACT.Square)
-
-        def scatter(k):
-            nc.vector.scalar_tensor_tensor(
-                neg_dx[k][:], vp2[k][:], 1.0, c0[k // 2][:, (k % 2) * I : (k % 2 + 1) * I], ALU.subtract, ALU.mult
+        def slot_gradient(k, tag=None):
+            neg_gs = sb("neg_gs%d" % k, [P, I], F32, tag)
+            nc.vector.tensor_tensor(
+                neg_gs[:], c0[k // 2][:, (k % 2) * I : (k % 2 + 1) * I], neg_slope[k][:], ALU.mult
             )
-            nc.vector.tensor_tensor(windows[k][:].indirect(offsets[:]), neg_dx[k][:], neg_sg[:], ALU.mult)
+            return neg_gs
 
-        faded_t = [sb("faded_t%d" % a, [P, BLOCKS, 2 * P], F32) for a in range(2)]
+        def scatter(k, neg_gs):
+            nc.vector.tensor_copy(windows[k][:].indirect(offsets[:]), neg_gs[:])
 
-        def fade_pair(a):
-            for cc in range(BLOCKS // 2):
-                stage = bank(4 + cc % 2, "stage%d_%d" % (a, cc))
-                for c2 in range(2):
-                    c = 2 * cc + c2
-                    for k2 in range(2):
-                        nc.tensor.transpose(
-                            stage[:, (2 * c2 + k2) * P : (2 * c2 + k2 + 1) * P],
-                            old_pair[a][:, k2, c * P : (c + 1) * P],
-                            ident[:],
-                        )
-                for c2 in range(2):
-                    c = 2 * cc + c2
-                    nc.scalar.activation(
-                        faded_t[a][:, c, :], stage[:, 2 * c2 * P : 2 * (c2 + 1) * P], ACT.Copy, scale=cols[:, c : c + 1]
-                    )
+        def store(k, h, result):
+            (nc.scalar if k % 2 else nc.sync).dma_start(out[k * P : (k + 1) * P, h * BANK : (h + 1) * BANK], result[:])
 
-        def finish(k):
+        def fade_on_gpsimd(k, halves):
             for h in range(2):
-                faded = bank(2 * (k % 2) + h, "faded%d_%d" % (k, h))
-                for c4 in range(4):
-                    nc.tensor.transpose(
-                        faded[:, c4 * P : (c4 + 1) * P],
-                        faded_t[k // 2][:, 4 * h + c4, (k % 2) * P : (k % 2 + 1) * P],
-                        ident[:],
-                    )
-                result = sb("result%d_%d" % (k, h), [P, BANK], F32)
-                nc.vector.tensor_tensor(result[:], faded[:], windows[k][:, h * BANK : (h + 1) * BANK], ALU.add)
-                nc.sync.dma_start(out[k * P : (k + 1) * P, h * BANK : (h + 1) * BANK], result[:])
+                half = slice(h * BANK, (h + 1) * BANK)
+                nc.gpsimd.tensor_tensor(halves[h], old_tile[k][:, half], fade_rows[:, half], ALU.mult)
+            return halves
 
-        prepare(0)
+        def finish_on_gpsimd(k, halves):
+            for h in range(2):
+                result = sb("result%d_%d" % (k, h), [P, BANK], F32)
+                nc.gpsimd.tensor_tensor(result[:], halves[h], windows[k][:, h * BANK : (h + 1) * BANK], ALU.subtract)
+                store(k, h, result)
+
         product(0)
         product(1)
-        scatter(0)
-        prepare(1)
-        scatter(1)
-        fade_pair(0)
+        gather(2)
+        neg_gs0 = slot_gradient(0, "val_pool2")
         cast_grows(1)
-        quantise_grows(1)
+        quantise_grows(1, "val_pool1")
+        scatter(0, neg_gs0)
+        first = sb("faded0", [P, T], F32, "w_bf")
+        faded0 = fade_on_gpsimd(0, [first[:, 0:BANK], first[:, BANK:T]])
         product(2)
         product(3)
         prepare(2)
-        finish(0)
+        gather(3)
+        neg_gs = [slot_gradient(1, "val_pool3"), slot_gradient(2)]
+        scatter(1, neg_gs[0])
+        finish_on_gpsimd(0, faded0)
+        faded2 = fade_on_gpsimd(2, [sb("faded2_%d" % h, [P, BANK], F32, LATE_TAGS[h])[:] for h in range(2)])
         prepare(3)
-        scatter(2)
-        fade_pair(1)
-        finish(1)
-        scatter(3)
-        finish(2)
-        finish(3)
+        neg_gs.append(slot_gradient(3))
+        scatter(2, neg_gs[1])
+        finish_on_gpsimd(2, faded2)
+        scatter(3, neg_gs[2])
+
+        faded_t = sb("faded_t", [P, BLOCKS, 2 * P], F32)
+        for cc in range(BLOCKS // 2):
+            stage = bank((7, 1, 0, 7)[cc], "stage%d" % cc)
+            for c2 in range(2):
+                c = 2 * cc + c2
+                for k2 in range(2):
+                    nc.tensor.transpose(
+                        stage[:, (2 * c2 + k2) * P : (2 * c2 + k2 + 1) * P], old_pair[:, k2, c * P : (c + 1) * P], ident[:]
+                    )
+            for c2 in range(2):
+                c = 2 * cc + c2
+                nc.scalar.activation(
+                    faded_t[:, c, :], stage[:, 2 * c2 * P : 2 * (c2 + 1) * P], ACT.Copy, scale=cols[:, c : c + 1]
+                )
+
+
+        for h in range(2):
+            stage = bank(h, "gf_stage%d" % h)
+            for c4 in range(4):
+                c = 4 * h + c4
+                nc.tensor.transpose(stage[:, c4 * P : (c4 + 1) * P], windows[1][:, c * P : (c + 1) * P], ident[:])
+            gf_t = sb("gf_t%d" % h, [P, BANK], F32)
+            nc.scalar.activation(gf_t[:], stage[:], ACT.Copy, scale=-1.0)
+            total = bank(2 + h, "total%d" % h)
+            for c4 in range(4):
+                block = total[:, c4 * P : (c4 + 1) * P]
+                nc.tensor.matmul(block, faded_t[:, 4 * h + c4, 0:P], ident[:], start=c4 == 0, stop=False, is_transpose=True)
+            for c4 in range(4):
+                block = total[:, c4 * P : (c4 + 1) * P]
+                nc.tensor.matmul(block, gf_t[:, c4 * P : (c4 + 1) * P], ident[:], start=False, stop=c4 == 3, is_transpose=True)
+            result = sb("result1_%d" % h, [P, BANK], F32)
+            nc.scalar.copy(result[:], total[:])
+            store(1, h, result)
+
+        faded3 = [bank(b, "faded3_%d" % b) for b in (4, 7)]
+        for c in range(BLOCKS):
+            nc.tensor.transpose(faded3[c // 4][:, (c % 4) * P : (c % 4 + 1) * P], faded_t[:, c, P : 2 * P], ident[:])
+
+        last = sb("result3", [P, T], F32, "gf_t1")
+        for h in range(2):
+            half = slice(h * BANK, (h + 1) * BANK)
+            nc.vector.tensor_tensor(last[:, half], faded3[h][:], windows[3][:, half], ALU.subtract)
+            store(3, h, last[:, half])

@@ -20,10 +20,15 @@ AX = mybir.AxisListType
 
 P = 128
 PACK = 4
+RUN = 4
 TILES = E // P
 BLOCKS = T // P
 BANK = 512
-LATE_TAGS = ("neg_slope0", "vp2_1")
+PER_BANK = BANK // P
+HALF = 256
+S_HALF = HALF // PACK
+S_VECTOR = 40
+FADE_ROW, GAIN_ROW, SG_ROW, END_ROW = 0, 8, 12, 14
 
 
 def tile_attend_bvtanh_s_kernel(tc, query, qs, grows, vals, keys_words, keys_scales, gain, sg, old, fade, offs, out):
@@ -35,13 +40,21 @@ def tile_attend_bvtanh_s_kernel(tc, query, qs, grows, vals, keys_words, keys_sca
         def sb(name, shape, dtype, tag=None):
             return keep.tile(shape, dtype, name=name, tag=tag or name, align_bytes=64)
 
-        def bank(b, name):
-            return psum.tile([P, BANK], F32, name=name, tag="bank%d" % b)
+        def bank(number, name):
+            return psum.tile([P, BANK], F32, name=name, tag="bank%d" % number)
+
+        def block(n):
+            return slice(n * P, (n + 1) * P)
+
+        def half(h):
+            return slice(h * BANK, (h + 1) * BANK)
 
         key_planes = sb("key_planes", [P, T], U8)
-        nc.vector.memset(key_planes[:].bitcast(I32), 0)
+        nc.gpsimd.memset(key_planes[:].bitcast(I32), 0)
         rows = sb("rows", [P, P], F32)
-        nc.vector.memset(rows[:], 0.0)
+        nc.gpsimd.memset(rows[:], 0.0)
+        zero = sb("zero", [P, 1], F32)
+        nc.gpsimd.memset(zero[:], 0.0)
         ident = sb("ident", [P, P], F32)
         make_identity(nc, ident[:])
 
@@ -54,39 +67,40 @@ def tile_attend_bvtanh_s_kernel(tc, query, qs, grows, vals, keys_words, keys_sca
                 key_planes[32 * quad : 32 * quad + 4, :].bitcast(I32),
                 keys_scales[0, 4 * quad : 4 * quad + 4, :].bitcast(I32),
             )
-        qs_cols = sb("qs_cols", [P, PACK], F32)
-        warm_out = sb("warm_out", [P, 8], F32)
-        nc.scalar.activation(warm_out[:], ident[:, 0:8], ACT.Exp)
+        one = sb("one", [P, 1], F32)
+        nc.scalar.activation(one[:], zero[:], ACT.Exp)
+
         query_rows = query.rearrange("(p j) q -> p j q", j=PACK)
         grows_rows = grows.rearrange("(p j) e -> p j e", j=PACK)
-        q_raw = [sb("q_raw%d" % h, [P, PACK, Q // 2], F32) for h in range(2)]
-        g_raw = [sb("g_raw%d" % h, [P, PACK, E // 2], F32) for h in range(2)]
+        q_raw = [sb("q_raw%d" % h, [P, PACK, HALF], F32) for h in range(2)]
+        g_raw = [sb("g_raw%d" % h, [P, PACK, HALF], F32) for h in range(2)]
+        qs_cols = sb("qs_cols", [P, PACK], F32)
         val_pool = [sb("val_pool%d" % k, [P, T], F32) for k in range(TILES)]
-        old_tile = {k: sb("old_tile%d" % k, [P, T], F32) for k in (0, 2)}
+        old_tile = {k: sb("old_tile%d" % k, [P, T], F32) for k in (1, 2)}
+        old_pair = sb("old_pair", [P, 2, T], F32)
 
         def load_vals(k):
-            nc.sync.dma_start(val_pool[k][:], vals[k * P : (k + 1) * P, :])
+            nc.sync.dma_start(val_pool[k][:], vals[block(k), :])
 
         for h in range(2):
-            nc.sync.dma_start(q_raw[h][:], query_rows[:, :, h * 256 : (h + 1) * 256])
-        nc.sync.dma_start(g_raw[0][:], grows_rows[:, :, 0:256])
-        nc.sync.dma_start(rows[0:8, :], fade.rearrange("o (c n) -> (o c) n", n=P))
-        nc.sync.dma_start(rows[8:12, :], gain.rearrange("(k n) o -> k (n o)", n=P))
-        nc.sync.dma_start(rows[12:14, :], sg.rearrange("o (c n) -> (o c) n", n=P))
+            nc.sync.dma_start(q_raw[h][:], query_rows[:, :, h * HALF : (h + 1) * HALF])
+        nc.sync.dma_start(g_raw[0][:], grows_rows[:, :, 0:HALF])
+        nc.sync.dma_start(rows[FADE_ROW:GAIN_ROW, :], fade.rearrange("o (c n) -> (o c) n", n=P))
+        nc.sync.dma_start(rows[GAIN_ROW:SG_ROW, :], gain.rearrange("(k n) o -> k (n o)", n=P))
+        nc.sync.dma_start(rows[SG_ROW:END_ROW, :], sg.rearrange("o (c n) -> (o c) n", n=P))
         nc.sync.dma_start(qs_cols[:], qs.rearrange("(p r) o -> p (r o)", r=PACK))
         load_vals(0)
         load_vals(1)
-        nc.sync.dma_start(g_raw[1][:], grows_rows[:, :, 256:512])
+        nc.sync.dma_start(g_raw[1][:], grows_rows[:, :, HALF : 2 * HALF])
         load_vals(2)
+        nc.sync.dma_start(old_tile[1][:], old[block(1), :])
+        nc.sync.dma_start(old_pair[:], old.rearrange("(k p) t -> p k t", p=P)[:, 0:TILES:3, :])
+        nc.sync.dma_start(old_tile[2][:], old[block(2), :])
         load_vals(3)
-        nc.sync.dma_start(old_tile[0][:], old[0 * P : 1 * P, :])
-        old_pair = sb("old_pair", [P, 2, T], F32)
-        nc.sync.dma_start(old_pair[:], old.rearrange("(a b p) t -> p a b t", p=P, b=2)[:, :, 1, :])
-        nc.sync.dma_start(old_tile[2][:], old[2 * P : 3 * P, :])
 
         windows = [sb("window%d" % k, [P, T], F32) for k in range(3)]
         nc.vector.memset(windows[0][:], 0.0)
-        for k in range(1, 3):
+        for k in (1, 2):
             nc.gpsimd.memset(windows[k][:], 0.0)
         windows.append(windows[0])
 
@@ -96,33 +110,36 @@ def tile_attend_bvtanh_s_kernel(tc, query, qs, grows, vals, keys_words, keys_sca
         nc.vector.tensor_copy(planes_g[:], key_planes[:].indirect(offsets[:]))
 
         q_bf = sb("q_bf", [P, PACK, P, PACK], BF16)
-        for h, lo, hi, copy in ((0, 0, 64, nc.vector.tensor_copy), (1, 0, 40, nc.vector.tensor_copy), (1, 40, 64, nc.scalar.copy)):
+        for h, lo, hi, copy in (
+            (0, 0, S_HALF, nc.vector.tensor_copy),
+            (1, 0, S_VECTOR, nc.vector.tensor_copy),
+            (1, S_VECTOR, S_HALF, nc.scalar.copy),
+        ):
             copy(
-                q_bf[:, :, 64 * h + lo : 64 * h + hi, :].rearrange("p r s j -> p s r j"),
+                q_bf[:, :, S_HALF * h + lo : S_HALF * h + hi, :].rearrange("p r s j -> p s r j"),
                 q_raw[h][:].rearrange("p j (s r) -> p s r j", r=PACK)[:, lo:hi],
             )
         q_codes = sb("q_codes", [P, Q], U32)
         q_planes = sb("q_planes", [P, Q], U8)
-        for lo, hi in ((0, 1), (1, 2), (2, 4)):
+        for lo, hi in ((0, 1), (1, 2), (2, PACK)):
             nc.vector.quantize_mx(
                 out=q_codes[:, P * lo : P * hi].bitcast(FP8X4),
                 scales=q_planes[:, P * lo : P * hi],
                 in_=q_bf[:, lo:hi, :, :].rearrange("p r s j -> p (r s j)"),
             )
 
-        g_bf = []
+        g_bf = [sb("g_bf%d" % h, [P, HALF, PACK], BF16) for h in range(2)]
         g_codes, g_planes = [], []
 
-        def cast_grows(h, tag=None):
-            g_bf.append(sb("g_bf%d" % h, [P, E // 2, PACK], BF16, tag))
+        def cast_grows(h):
             nc.scalar.copy(
-                g_bf[h][:].rearrange("p (c i) j -> p c j i", i=4),
-                g_raw[h][:].rearrange("p j (c i) -> p c j i", i=4),
+                g_bf[h][:].rearrange("p (c i) j -> p c j i", i=RUN),
+                g_raw[h][:].rearrange("p j (c i) -> p c j i", i=RUN),
             )
 
         def quantise_grows(h, tag=None):
-            g_codes.append(sb("g_codes%d" % h, [P, E // 2], U32, tag))
-            g_planes.append(sb("g_planes%d" % h, [P, E // 2], U8))
+            g_codes.append(sb("g_codes%d" % h, [P, HALF], U32, tag))
+            g_planes.append(sb("g_planes%d" % h, [P, HALF], U8))
             nc.vector.quantize_mx(
                 out=g_codes[h][:].bitcast(FP8X4),
                 scales=g_planes[h][:],
@@ -138,8 +155,8 @@ def tile_attend_bvtanh_s_kernel(tc, query, qs, grows, vals, keys_words, keys_sca
             scores = bank(r, "scores%d" % r)
             nc.tensor.matmul_mx(
                 out=scores[:, 0:I],
-                lhsT=q_codes[:, r * P : (r + 1) * P].bitcast(FP8X4),
-                lhsT_scale=q_planes[:, r * P : (r + 1) * P],
+                lhsT=q_codes[:, block(r)].bitcast(FP8X4),
+                lhsT_scale=q_planes[:, block(r)],
                 rhs=keys_g[:].bitcast(FP4X4),
                 rhs_scale=planes_g[:],
                 start=True,
@@ -154,14 +171,17 @@ def tile_attend_bvtanh_s_kernel(tc, query, qs, grows, vals, keys_words, keys_sca
         nc.tensor.transpose(turned[:, 0:P], rows[:], ident[:])
         cols = sb("cols", [P, 16], F32)
         nc.scalar.copy(cols[:], turned[:, 0:16])
+
+        def spread_column(dst, n):
+            nc.tensor.transpose(dst, cols[:, n : n + 1].to_broadcast([P, P]), ident[:])
+
         sg_rows = bank(5, "sg_rows")
-        for c in range(2):
-            nc.tensor.transpose(sg_rows[:, c * P : (c + 1) * P], cols[:, 12 + c : 13 + c].to_broadcast([P, P]), ident[:])
+        for c in range(I // P):
+            spread_column(sg_rows[:, block(c)], SG_ROW + c)
 
-        picked = []
+        picked = [sb("picked%d" % k, [P, I], F32) for k in range(TILES)]
 
-        def gather(k, tag=None):
-            picked.append(sb("picked%d" % k, [P, I], F32, tag))
+        def gather(k):
             nc.vector.tensor_copy(picked[k][:], val_pool[k][:].indirect(offsets[:]))
 
         quantise_grows(0)
@@ -176,134 +196,147 @@ def tile_attend_bvtanh_s_kernel(tc, query, qs, grows, vals, keys_words, keys_sca
             )
         w_bf = sb("w_bf", [P, I, PACK], BF16)
         nc.vector.tensor_copy(
-            w_bf[:].rearrange("p (c i) r -> p c r i", i=4), w_lin[:].rearrange("p r (c i) -> p c r i", i=4)
+            w_bf[:].rearrange("p (c i) r -> p c r i", i=RUN), w_lin[:].rearrange("p r (c i) -> p c r i", i=RUN)
         )
 
-        neg_slope = []
+        neg_slope = [sb("neg_slope%d" % k, [P, I], F32) for k in range(TILES)]
 
-        def prepare(k, tag=None):
+        def slope(k, tag=None):
             vp = sb("vp%d" % k, [P, I], F32, tag)
-            nc.scalar.activation(vp[:], picked[k][:], ACT.Tanh, scale=cols[:, 8 + k : 9 + k])
-            vp2 = sb("vp2_%d" % k, [P, I], F32)
-            nc.scalar.activation(vp2[:], vp[:], ACT.Square)
-            neg_slope.append(sb("neg_slope%d" % k, [P, I], F32))
-            nc.vector.scalar_tensor_tensor(neg_slope[k][:], vp2[:], 1.0, sg_rows[:, 0:I], ALU.subtract, ALU.mult)
+            nc.scalar.activation(vp[:], picked[k][:], ACT.Tanh, scale=cols[:, GAIN_ROW + k : GAIN_ROW + k + 1])
+            vp_sq = sb("vp_sq%d" % k, [P, I], F32)
+            nc.scalar.activation(vp_sq[:], vp[:], ACT.Square)
+            nc.vector.scalar_tensor_tensor(neg_slope[k][:], vp_sq[:], one[:], sg_rows[:, 0:I], ALU.subtract, ALU.mult)
 
-        prepare(0)
+        slope(0)
         w_codes = sb("w_codes", [P, I], U32)
         w_planes = sb("w_planes", [P, I], U8)
-        nc.vector.quantize_mx(out=w_codes[:].bitcast(FP8X4), scales=w_planes[:], in_=w_bf[:].rearrange("p i r -> p (i r)"))
+        nc.vector.quantize_mx(
+            out=w_codes[:].bitcast(FP8X4), scales=w_planes[:], in_=w_bf[:].rearrange("p i r -> p (i r)")
+        )
+        slope(1)
 
-        prepare(1)
         fade_rows = sb("fade_rows", [P, T], F32, "vp1")
         for h in range(2):
             spread = bank(6 + h, "spread%d" % h)
-            for c4 in range(4):
-                c = 4 * h + c4
-                nc.tensor.transpose(spread[:, c4 * P : (c4 + 1) * P], cols[:, c : c + 1].to_broadcast([P, P]), ident[:])
-            nc.scalar.copy(fade_rows[:, h * BANK : (h + 1) * BANK], spread[:])
+            for c in range(PER_BANK):
+                spread_column(spread[:, block(c)], FADE_ROW + PER_BANK * h + c)
+            nc.scalar.copy(fade_rows[:, half(h)], spread[:])
 
-        c0 = [bank(4, "c0_0"), bank(6, "c0_1")]
+        c0_banks = [bank(4, "c0_0"), bank(6, "c0_1")]
+
+        def c0(k):
+            return c0_banks[k // 2][:, (k % 2) * I : (k % 2 + 1) * I]
 
         def product(k):
             nc.tensor.matmul_mx(
-                out=c0[k // 2][:, (k % 2) * I : (k % 2 + 1) * I],
-                lhsT=g_codes[k // 2][:, (k % 2) * P : (k % 2 + 1) * P].bitcast(FP8X4),
-                lhsT_scale=g_planes[k // 2][:, (k % 2) * P : (k % 2 + 1) * P],
+                out=c0(k),
+                lhsT=g_codes[k // 2][:, block(k % 2)].bitcast(FP8X4),
+                lhsT_scale=g_planes[k // 2][:, block(k % 2)],
                 rhs=w_codes[:].bitcast(FP8X4),
                 rhs_scale=w_planes[:],
                 start=True,
                 stop=True,
             )
 
+        neg_gs = {}
+
         def slot_gradient(k, tag=None):
-            neg_gs = sb("neg_gs%d" % k, [P, I], F32, tag)
-            nc.vector.tensor_tensor(
-                neg_gs[:], c0[k // 2][:, (k % 2) * I : (k % 2 + 1) * I], neg_slope[k][:], ALU.mult
-            )
-            return neg_gs
+            neg_gs[k] = sb("neg_gs%d" % k, [P, I], F32, tag)
+            nc.vector.tensor_tensor(neg_gs[k][:], c0(k), neg_slope[k][:], ALU.mult)
 
-        def scatter(k, neg_gs):
-            nc.vector.tensor_copy(windows[k][:].indirect(offsets[:]), neg_gs[:])
+        def scatter(k):
+            nc.vector.tensor_copy(windows[k][:].indirect(offsets[:]), neg_gs[k][:])
 
-        def store(k, h, result):
-            (nc.scalar if k % 2 else nc.sync).dma_start(out[k * P : (k + 1) * P, h * BANK : (h + 1) * BANK], result[:])
+        def store(queue, k, h, result):
+            queue.dma_start(out[block(k), half(h)], result)
 
-        def fade_on_gpsimd(k, halves):
+        def fade_on_gpsimd(k, faded):
             for h in range(2):
-                half = slice(h * BANK, (h + 1) * BANK)
-                nc.gpsimd.tensor_tensor(halves[h], old_tile[k][:, half], fade_rows[:, half], ALU.mult)
-            return halves
+                nc.gpsimd.tensor_tensor(faded[h], old_tile[k][:, half(h)], fade_rows[:, half(h)], ALU.mult)
 
-        def finish_on_gpsimd(k, halves):
+        def finish_on_gpsimd(k, faded, tag):
+            result = sb("result%d" % k, [P, T], F32, tag)
             for h in range(2):
-                result = sb("result%d_%d" % (k, h), [P, BANK], F32)
-                nc.gpsimd.tensor_tensor(result[:], halves[h], windows[k][:, h * BANK : (h + 1) * BANK], ALU.subtract)
-                store(k, h, result)
+                nc.gpsimd.tensor_tensor(result[:, half(h)], faded[h], windows[k][:, half(h)], ALU.subtract)
+                store(nc.sync, k, h, result[:, half(h)])
 
         product(0)
         product(1)
         gather(2)
-        neg_gs0 = slot_gradient(0, "val_pool2")
+        slot_gradient(0, "val_pool2")
         cast_grows(1)
         quantise_grows(1, "val_pool1")
-        scatter(0, neg_gs0)
-        first = sb("faded0", [P, T], F32, "w_bf")
-        faded0 = fade_on_gpsimd(0, [first[:, 0:BANK], first[:, BANK:T]])
+        scatter(0)
+        faded1_tile = sb("faded1", [P, T], F32, "g_bf1")
+        faded1 = [faded1_tile[:, half(h)] for h in range(2)]
+        fade_on_gpsimd(1, faded1)
+        faded2 = [sb("faded2_%d" % h, [P, BANK], F32, ("neg_slope0", "vp_sq1")[h])[:] for h in range(2)]
+        fade_on_gpsimd(2, faded2)
         product(2)
         product(3)
-        prepare(2)
+        slope(2)
         gather(3)
-        neg_gs = [slot_gradient(1, "val_pool3"), slot_gradient(2)]
-        scatter(1, neg_gs[0])
-        finish_on_gpsimd(0, faded0)
-        faded2 = fade_on_gpsimd(2, [sb("faded2_%d" % h, [P, BANK], F32, LATE_TAGS[h])[:] for h in range(2)])
-        prepare(3)
-        neg_gs.append(slot_gradient(3))
-        scatter(2, neg_gs[1])
-        finish_on_gpsimd(2, faded2)
-        scatter(3, neg_gs[2])
+        slot_gradient(1)
+        slot_gradient(2, "val_pool3")
+        scatter(1)
+        finish_on_gpsimd(1, faded1, "old_tile2")
 
-        faded_t = sb("faded_t", [P, BLOCKS, 2 * P], F32)
-        for cc in range(BLOCKS // 2):
-            stage = bank((7, 1, 0, 7)[cc], "stage%d" % cc)
-            for c2 in range(2):
-                c = 2 * cc + c2
-                for k2 in range(2):
-                    nc.tensor.transpose(
-                        stage[:, (2 * c2 + k2) * P : (2 * c2 + k2 + 1) * P], old_pair[:, k2, c * P : (c + 1) * P], ident[:]
-                    )
-            for c2 in range(2):
-                c = 2 * cc + c2
+        faded_t = sb("faded_t", [P, BLOCKS, 2, P], F32)
+        for step, number in enumerate((7, 1, 0, 7)):
+            stage = bank(number, "stage%d" % step)
+            for b in range(2):
+                for n in range(2):
+                    nc.tensor.transpose(stage[:, block(2 * b + n)], old_pair[:, n, block(2 * step + b)], ident[:])
+            for b in range(2):
+                c = 2 * step + b
                 nc.scalar.activation(
-                    faded_t[:, c, :], stage[:, 2 * c2 * P : 2 * (c2 + 1) * P], ACT.Copy, scale=cols[:, c : c + 1]
+                    faded_t[:, c, :, :].rearrange("p n e -> p (n e)"),
+                    stage[:, 2 * b * P : 2 * (b + 1) * P],
+                    ACT.Copy,
+                    scale=cols[:, FADE_ROW + c : FADE_ROW + c + 1],
                 )
 
+        slope(3, "old_pair")
+        slot_gradient(3)
+        scatter(2)
+        finish_on_gpsimd(2, faded2, "g_bf1")
 
         for h in range(2):
-            stage = bank(h, "gf_stage%d" % h)
-            for c4 in range(4):
-                c = 4 * h + c4
-                nc.tensor.transpose(stage[:, c4 * P : (c4 + 1) * P], windows[1][:, c * P : (c + 1) * P], ident[:])
+            gf_stage = bank(1 - h, "gf_stage%d" % h)
+            for c in range(PER_BANK):
+                nc.tensor.transpose(gf_stage[:, block(c)], windows[0][:, block(PER_BANK * h + c)], ident[:])
             gf_t = sb("gf_t%d" % h, [P, BANK], F32)
-            nc.scalar.activation(gf_t[:], stage[:], ACT.Copy, scale=-1.0)
+            nc.scalar.activation(gf_t[:], gf_stage[:], ACT.Copy, scale=-1.0)
             total = bank(2 + h, "total%d" % h)
-            for c4 in range(4):
-                block = total[:, c4 * P : (c4 + 1) * P]
-                nc.tensor.matmul(block, faded_t[:, 4 * h + c4, 0:P], ident[:], start=c4 == 0, stop=False, is_transpose=True)
-            for c4 in range(4):
-                block = total[:, c4 * P : (c4 + 1) * P]
-                nc.tensor.matmul(block, gf_t[:, c4 * P : (c4 + 1) * P], ident[:], start=False, stop=c4 == 3, is_transpose=True)
-            result = sb("result1_%d" % h, [P, BANK], F32)
-            nc.scalar.copy(result[:], total[:])
-            store(1, h, result)
+            for c in range(PER_BANK):
+                nc.tensor.matmul(
+                    total[:, block(c)],
+                    faded_t[:, PER_BANK * h + c, 0, :],
+                    ident[:],
+                    start=c == 0,
+                    stop=False,
+                    is_transpose=True,
+                )
+            for c in range(PER_BANK):
+                nc.tensor.matmul(
+                    total[:, block(c)],
+                    gf_t[:, block(c)],
+                    ident[:],
+                    start=False,
+                    stop=c == PER_BANK - 1,
+                    is_transpose=True,
+                )
+            result0 = sb("result0_%d" % h, [P, BANK], F32)
+            nc.scalar.copy(result0[:], total[:])
+            store(nc.sync, 0, h, result0[:])
 
-        faded3 = [bank(b, "faded3_%d" % b) for b in (4, 7)]
+        scatter(3)
+
+        faded3 = [bank(1 - h, "faded3_%d" % h) for h in range(2)]
         for c in range(BLOCKS):
-            nc.tensor.transpose(faded3[c // 4][:, (c % 4) * P : (c % 4 + 1) * P], faded_t[:, c, P : 2 * P], ident[:])
-
-        last = sb("result3", [P, T], F32, "gf_t1")
+            nc.tensor.transpose(faded3[c // PER_BANK][:, block(c % PER_BANK)], faded_t[:, c, 1, :], ident[:])
+        result3 = sb("result3", [P, T], F32, "gf_t1")
         for h in range(2):
-            half = slice(h * BANK, (h + 1) * BANK)
-            nc.vector.tensor_tensor(last[:, half], faded3[h][:], windows[3][:, half], ALU.subtract)
-            store(3, h, last[:, half])
+            nc.vector.tensor_tensor(result3[:, half(h)], faded3[h][:], windows[3][:, half(h)], ALU.subtract)
+            store(nc.scalar, 3, h, result3[:, half(h)])

@@ -29,6 +29,7 @@ HALF = 256
 S_HALF = HALF // PACK
 S_VECTOR = 40
 FADE_ROW, GAIN_ROW, SG_ROW, END_ROW = 0, 8, 12, 14
+COLS = 16
 
 
 def tile_attend_bvtanh_s_kernel(tc, query, qs, grows, vals, keys_words, keys_scales, gain, sg, old, fade, offs, out):
@@ -93,10 +94,10 @@ def tile_attend_bvtanh_s_kernel(tc, query, qs, grows, vals, keys_words, keys_sca
         load_vals(1)
         nc.sync.dma_start(g_raw[1][:], grows_rows[:, :, HALF : 2 * HALF])
         load_vals(2)
-        nc.sync.dma_start(old_tile[1][:], old[block(1), :])
-        nc.sync.dma_start(old_pair[:], old.rearrange("(k p) t -> p k t", p=P)[:, 0:TILES:3, :])
-        nc.sync.dma_start(old_tile[2][:], old[block(2), :])
         load_vals(3)
+        nc.sync.dma_start(old_tile[1][:], old[block(1), :])
+        nc.sync.dma_start(old_pair[:], old.rearrange("(k p) t -> p k t", p=P)[:, 0 : TILES : TILES - 1, :])
+        nc.sync.dma_start(old_tile[2][:], old[block(2), :])
 
         windows = [sb("window%d" % k, [P, T], F32) for k in range(3)]
         nc.vector.memset(windows[0][:], 0.0)
@@ -169,8 +170,8 @@ def tile_attend_bvtanh_s_kernel(tc, query, qs, grows, vals, keys_words, keys_sca
 
         turned = bank(4, "turned")
         nc.tensor.transpose(turned[:, 0:P], rows[:], ident[:])
-        cols = sb("cols", [P, 16], F32)
-        nc.scalar.copy(cols[:], turned[:, 0:16])
+        cols = sb("cols", [P, COLS], F32)
+        nc.scalar.copy(cols[:], turned[:, 0:COLS])
 
         def spread_column(dst, n):
             nc.tensor.transpose(dst, cols[:, n : n + 1].to_broadcast([P, P]), ident[:])
@@ -199,14 +200,19 @@ def tile_attend_bvtanh_s_kernel(tc, query, qs, grows, vals, keys_words, keys_sca
             w_bf[:].rearrange("p (c i) r -> p c r i", i=RUN), w_lin[:].rearrange("p r (c i) -> p c r i", i=RUN)
         )
 
-        neg_slope = [sb("neg_slope%d" % k, [P, I], F32) for k in range(TILES)]
+        vp_sq = [sb("vp_sq%d" % k, [P, I], F32) for k in range(TILES)]
+        neg_slope = [sb("neg_slope%d" % k, [P, I], F32) for k in range(2)]
 
-        def slope(k, tag=None):
-            vp = sb("vp%d" % k, [P, I], F32, tag)
+        def tanh_squared(k):
+            vp = sb("vp%d" % k, [P, I], F32)
             nc.scalar.activation(vp[:], picked[k][:], ACT.Tanh, scale=cols[:, GAIN_ROW + k : GAIN_ROW + k + 1])
-            vp_sq = sb("vp_sq%d" % k, [P, I], F32)
-            nc.scalar.activation(vp_sq[:], vp[:], ACT.Square)
-            nc.vector.scalar_tensor_tensor(neg_slope[k][:], vp_sq[:], one[:], sg_rows[:, 0:I], ALU.subtract, ALU.mult)
+            nc.scalar.activation(vp_sq[k][:], vp[:], ACT.Square)
+
+        def slope(k):
+            tanh_squared(k)
+            nc.vector.scalar_tensor_tensor(
+                neg_slope[k][:], vp_sq[k][:], one[:], sg_rows[:, 0:I], ALU.subtract, ALU.mult
+            )
 
         slope(0)
         w_codes = sb("w_codes", [P, I], U32)
@@ -231,19 +237,46 @@ def tile_attend_bvtanh_s_kernel(tc, query, qs, grows, vals, keys_words, keys_sca
         def product(k):
             nc.tensor.matmul_mx(
                 out=c0(k),
-                lhsT=g_codes[k // 2][:, block(k % 2)].bitcast(FP8X4),
-                lhsT_scale=g_planes[k // 2][:, block(k % 2)],
+                lhsT=g_codes[0][:, block(k)].bitcast(FP8X4),
+                lhsT_scale=g_planes[0][:, block(k)],
                 rhs=w_codes[:].bitcast(FP8X4),
                 rhs_scale=w_planes[:],
                 start=True,
                 stop=True,
             )
 
+        def scaled_products():
+            by_slot = bank(5, "by_slot")
+            scaled = sb("scaled", [P, I // P, HALF], F32)
+            for c in range(I // P):
+                nc.tensor.matmul_mx(
+                    out=by_slot[:, c * HALF : (c + 1) * HALF],
+                    lhsT=w_codes[:, block(c)].bitcast(FP8X4),
+                    lhsT_scale=w_planes[:, block(c)],
+                    rhs=g_codes[1][:].bitcast(FP8X4),
+                    rhs_scale=g_planes[1][:],
+                    start=True,
+                    stop=True,
+                )
+            for c in range(I // P):
+                nc.scalar.activation(
+                    scaled[:, c, :],
+                    by_slot[:, c * HALF : (c + 1) * HALF],
+                    ACT.Copy,
+                    scale=cols[:, SG_ROW + c : SG_ROW + c + 1],
+                )
+            for k in (2, 3):
+                for c in range(I // P):
+                    nc.tensor.transpose(c0(k)[:, block(c)], scaled[:, c, block(k - 2)], ident[:])
+
         neg_gs = {}
 
         def slot_gradient(k, tag=None):
             neg_gs[k] = sb("neg_gs%d" % k, [P, I], F32, tag)
-            nc.vector.tensor_tensor(neg_gs[k][:], c0(k), neg_slope[k][:], ALU.mult)
+            if k < 2:
+                nc.vector.tensor_tensor(neg_gs[k][:], c0(k), neg_slope[k][:], ALU.mult)
+            else:
+                nc.vector.scalar_tensor_tensor(neg_gs[k][:], vp_sq[k][:], one[:], c0(k), ALU.subtract, ALU.mult)
 
         def scatter(k):
             nc.vector.tensor_copy(windows[k][:].indirect(offsets[:]), neg_gs[k][:])
@@ -255,16 +288,17 @@ def tile_attend_bvtanh_s_kernel(tc, query, qs, grows, vals, keys_words, keys_sca
             for h in range(2):
                 nc.gpsimd.tensor_tensor(faded[h], old_tile[k][:, half(h)], fade_rows[:, half(h)], ALU.mult)
 
-        def finish_on_gpsimd(k, faded, tag):
+        def finish_on_gpsimd(k, faded, halves, tag):
             result = sb("result%d" % k, [P, T], F32, tag)
-            for h in range(2):
+            for h in halves:
                 nc.gpsimd.tensor_tensor(result[:, half(h)], faded[h], windows[k][:, half(h)], ALU.subtract)
                 store(nc.sync, k, h, result[:, half(h)])
 
         product(0)
         product(1)
         gather(2)
-        slot_gradient(0, "val_pool2")
+        gather(3)
+        slot_gradient(0, "val_pool3")
         cast_grows(1)
         quantise_grows(1, "val_pool1")
         scatter(0)
@@ -273,14 +307,14 @@ def tile_attend_bvtanh_s_kernel(tc, query, qs, grows, vals, keys_words, keys_sca
         fade_on_gpsimd(1, faded1)
         faded2 = [sb("faded2_%d" % h, [P, BANK], F32, ("neg_slope0", "vp_sq1")[h])[:] for h in range(2)]
         fade_on_gpsimd(2, faded2)
-        product(2)
-        product(3)
-        slope(2)
-        gather(3)
+        scaled_products()
+        tanh_squared(2)
         slot_gradient(1)
-        slot_gradient(2, "val_pool3")
+        slot_gradient(2)
+        tanh_squared(3)
+        slot_gradient(3)
         scatter(1)
-        finish_on_gpsimd(1, faded1, "old_tile2")
+        finish_on_gpsimd(1, faded1, (0, 1), "old_tile2")
 
         faded_t = sb("faded_t", [P, BLOCKS, 2, P], F32)
         for step, number in enumerate((7, 1, 0, 7)):
@@ -297,10 +331,8 @@ def tile_attend_bvtanh_s_kernel(tc, query, qs, grows, vals, keys_words, keys_sca
                     scale=cols[:, FADE_ROW + c : FADE_ROW + c + 1],
                 )
 
-        slope(3, "old_pair")
-        slot_gradient(3)
         scatter(2)
-        finish_on_gpsimd(2, faded2, "g_bf1")
+        finish_on_gpsimd(2, faded2, (0,), "g_bf1")
 
         for h in range(2):
             gf_stage = bank(1 - h, "gf_stage%d" % h)
@@ -340,3 +372,7 @@ def tile_attend_bvtanh_s_kernel(tc, query, qs, grows, vals, keys_words, keys_sca
         for h in range(2):
             nc.vector.tensor_tensor(result3[:, half(h)], faded3[h][:], windows[3][:, half(h)], ALU.subtract)
             store(nc.scalar, 3, h, result3[:, half(h)])
+
+        result2_last = sb("result2_last", [P, BANK], F32, "window0")
+        nc.vector.tensor_tensor(result2_last[:], faded2[1], windows[2][:, half(1)], ALU.subtract)
+        store(nc.scalar, 2, 1, result2_last[:])

from contextlib import ExitStack

import concourse.mybir as mybir
from concourse.masks import make_identity

D, E, T, I, Q = 512, 512, 1024, 256, 512
FLOPS = 2 * D * Q * I + 2 * Q * E * I

F32 = mybir.dt.float32
BF16 = mybir.dt.bfloat16
I32 = mybir.dt.int32
U32 = mybir.dt.uint32
U16 = mybir.dt.uint16
U8 = mybir.dt.uint8
FP8X4 = mybir.dt.float8_e4m3fn_x4
FP4X4 = mybir.dt.float4_e2m1fn_x4
ALU = mybir.AluOpType
ACT = mybir.ActivationFunctionType
AX = mybir.AxisListType

P = 128
PACK = 4
RUN = 4
TILES = E // P
BLOCKS = T // P
BANK = 512
PER_BANK = BANK // P
HALF = 256
S_HALF = HALF // PACK
S_VECTOR = 40
FADE_ROW, GAIN_ROW, SG_ROW, END_ROW = 0, 8, 12, 14
COLS = 16


def tile_attend_bvtanh_s_kernel(tc, query, qs, grows, vals, keys_words, keys_scales, gain, sg, old, fade, offs, out):
    nc = tc.nc
    with ExitStack() as ctx:
        keep = ctx.enter_context(tc.tile_pool(name="keep", bufs=1))
        psum = ctx.enter_context(tc.psum_pool(name="psum", bufs=1))

        def sb(name, shape, dtype, tag=None):
            return keep.tile(shape, dtype, name=name, tag=tag or name, align_bytes=64)

        def bank(number, name):
            return psum.tile([P, BANK], F32, name=name, tag="bank%d" % number)

        def block(n):
            return slice(n * P, (n + 1) * P)

        def half(h):
            return slice(h * BANK, (h + 1) * BANK)

        key_planes = sb("key_planes", [P, T], U8)
        nc.gpsimd.memset(key_planes[:].bitcast(I32), 0)
        rows = sb("rows", [P, P], F32)
        nc.gpsimd.memset(rows[:], 0.0)
        zero = sb("zero", [P, 1], F32)
        nc.gpsimd.memset(zero[:], 0.0)
        ident = sb("ident", [P, P], F32)
        make_identity(nc, ident[:])

        offsets = sb("offsets", [P, I // 16], U16)
        nc.sync.dma_start(offsets[:], offs)
        key_words = sb("key_words", [P, T], U16)
        nc.sync.dma_start(key_words[:].bitcast(I32), keys_words[0].bitcast(I32))
        for quad in range(4):
            (nc.scalar if quad < 2 else nc.sync).dma_start(
                key_planes[32 * quad : 32 * quad + 4, :].bitcast(I32),
                keys_scales[0, 4 * quad : 4 * quad + 4, :].bitcast(I32),
            )
        one = sb("one", [P, 1], F32)
        nc.scalar.activation(one[:], zero[:], ACT.Exp)

        query_rows = query.rearrange("(p j) q -> p j q", j=PACK)
        grows_rows = grows.rearrange("(p j) e -> p j e", j=PACK)
        q_raw = [sb("q_raw%d" % h, [P, PACK, HALF], F32) for h in range(2)]
        g_raw = [sb("g_raw%d" % h, [P, PACK, HALF], F32) for h in range(2)]
        qs_cols = sb("qs_cols", [P, PACK], F32)
        val_pool = [sb("val_pool%d" % k, [P, T], F32) for k in range(TILES)]
        old_tile = {k: sb("old_tile%d" % k, [P, T], F32) for k in (1, 2)}
        old_pair = sb("old_pair", [P, 2, T], F32)

        def load_vals(k):
            nc.sync.dma_start(val_pool[k][:], vals[block(k), :])

        for h in range(2):
            nc.sync.dma_start(q_raw[h][:], query_rows[:, :, h * HALF : (h + 1) * HALF])
        nc.sync.dma_start(g_raw[0][:], grows_rows[:, :, 0:HALF])
        nc.sync.dma_start(rows[FADE_ROW:GAIN_ROW, :], fade.rearrange("o (c n) -> (o c) n", n=P))
        nc.sync.dma_start(rows[GAIN_ROW:SG_ROW, :], gain.rearrange("(k n) o -> k (n o)", n=P))
        nc.sync.dma_start(rows[SG_ROW:END_ROW, :], sg.rearrange("o (c n) -> (o c) n", n=P))
        nc.sync.dma_start(qs_cols[:], qs.rearrange("(p r) o -> p (r o)", r=PACK))
        load_vals(0)
        load_vals(1)
        nc.sync.dma_start(g_raw[1][:], grows_rows[:, :, HALF : 2 * HALF])
        load_vals(2)
        load_vals(3)
        nc.sync.dma_start(old_tile[1][:], old[block(1), :])
        nc.sync.dma_start(old_pair[:], old.rearrange("(k p) t -> p k t", p=P)[:, 0 : TILES : TILES - 1, :])
        nc.sync.dma_start(old_tile[2][:], old[block(2), :])

        windows = [sb("window%d" % k, [P, T], F32) for k in range(3)]
        nc.vector.memset(windows[0][:], 0.0)
        for k in (1, 2):
            nc.gpsimd.memset(windows[k][:], 0.0)
        windows.append(windows[0])

        keys_g = sb("keys_g", [P, I], U16)
        nc.vector.tensor_copy(keys_g[:], key_words[:].indirect(offsets[:]))
        planes_g = sb("planes_g", [P, I], U8)
        nc.vector.tensor_copy(planes_g[:], key_planes[:].indirect(offsets[:]))

        q_bf = sb("q_bf", [P, PACK, P, PACK], BF16)
        for h, lo, hi, copy in (
            (0, 0, S_HALF, nc.vector.tensor_copy),
            (1, 0, S_VECTOR, nc.vector.tensor_copy),
            (1, S_VECTOR, S_HALF, nc.scalar.copy),
        ):
            copy(
                q_bf[:, :, S_HALF * h + lo : S_HALF * h + hi, :].rearrange("p r s j -> p s r j"),
                q_raw[h][:].rearrange("p j (s r) -> p s r j", r=PACK)[:, lo:hi],
            )
        q_codes = sb("q_codes", [P, Q], U32)
        q_planes = sb("q_planes", [P, Q], U8)
        for lo, hi in ((0, 1), (1, 2), (2, PACK)):
            nc.vector.quantize_mx(
                out=q_codes[:, P * lo : P * hi].bitcast(FP8X4),
                scales=q_planes[:, P * lo : P * hi],
                in_=q_bf[:, lo:hi, :, :].rearrange("p r s j -> p (r s j)"),
            )

        g_bf = [sb("g_bf%d" % h, [P, HALF, PACK], BF16) for h in range(2)]
        g_codes, g_planes = [], []

        def cast_grows(h):
            nc.scalar.copy(
                g_bf[h][:].rearrange("p (c i) j -> p c j i", i=RUN),
                g_raw[h][:].rearrange("p j (c i) -> p c j i", i=RUN),
            )

        def quantise_grows(h, tag=None):
            g_codes.append(sb("g_codes%d" % h, [P, HALF], U32, tag))
            g_planes.append(sb("g_planes%d" % h, [P, HALF], U8))
            nc.vector.quantize_mx(
                out=g_codes[h][:].bitcast(FP8X4),
                scales=g_planes[h][:],
                in_=g_bf[h][:].rearrange("p e j -> p (e j)"),
            )

        cast_grows(0)

        neg_max = sb("neg_max", [P, PACK], F32)
        sums = sb("sums", [P, PACK], F32)
        probs = sb("probs", [P, PACK, I], F32)
        for r in range(PACK):
            scores = bank(r, "scores%d" % r)
            nc.tensor.matmul_mx(
                out=scores[:, 0:I],
                lhsT=q_codes[:, block(r)].bitcast(FP8X4),
                lhsT_scale=q_planes[:, block(r)],
                rhs=keys_g[:].bitcast(FP4X4),
                rhs_scale=planes_g[:],
                start=True,
                stop=True,
            )
            nc.vector.tensor_reduce(neg_max[:, r : r + 1], scores[:, 0:I], AX.X, ALU.max, negate=True)
            nc.scalar.activation(
                probs[:, r, :], scores[:, 0:I], ACT.Exp, bias=neg_max[:, r : r + 1], accum_out=sums[:, r : r + 1]
            )

        turned = bank(4, "turned")
        nc.tensor.transpose(turned[:, 0:P], rows[:], ident[:])
        cols = sb("cols", [P, COLS], F32)
        nc.scalar.copy(cols[:], turned[:, 0:COLS])

        def spread_column(dst, n):
            nc.tensor.transpose(dst, cols[:, n : n + 1].to_broadcast([P, P]), ident[:])

        sg_rows = bank(5, "sg_rows")
        for c in range(I // P):
            spread_column(sg_rows[:, block(c)], SG_ROW + c)

        picked = [sb("picked%d" % k, [P, I], F32) for k in range(TILES)]

        def gather(k):
            nc.vector.tensor_copy(picked[k][:], val_pool[k][:].indirect(offsets[:]))

        quantise_grows(0)
        gather(0)
        inv = sb("inv", [P, PACK], F32, "val_pool0")
        nc.vector.reciprocal(inv[:], sums[:])
        gather(1)
        w_lin = sb("w_lin", [P, PACK, I], BF16, "val_pool1")
        for r in range(PACK):
            nc.vector.tensor_scalar(
                w_lin[:, r, :], probs[:, r, :], inv[:, r : r + 1], qs_cols[:, r : r + 1], ALU.mult, ALU.mult
            )
        w_bf = sb("w_bf", [P, I, PACK], BF16)
        nc.vector.tensor_copy(
            w_bf[:].rearrange("p (c i) r -> p c r i", i=RUN), w_lin[:].rearrange("p r (c i) -> p c r i", i=RUN)
        )

        vp_sq = [sb("vp_sq%d" % k, [P, I], F32) for k in range(TILES)]
        neg_slope = [sb("neg_slope%d" % k, [P, I], F32) for k in range(2)]

        def tanh_squared(k):
            vp = sb("vp%d" % k, [P, I], F32)
            nc.scalar.activation(vp[:], picked[k][:], ACT.Tanh, scale=cols[:, GAIN_ROW + k : GAIN_ROW + k + 1])
            nc.scalar.activation(vp_sq[k][:], vp[:], ACT.Square)

        def slope(k):
            tanh_squared(k)
            nc.vector.scalar_tensor_tensor(
                neg_slope[k][:], vp_sq[k][:], one[:], sg_rows[:, 0:I], ALU.subtract, ALU.mult
            )

        slope(0)
        w_codes = sb("w_codes", [P, I], U32)
        w_planes = sb("w_planes", [P, I], U8)
        nc.vector.quantize_mx(
            out=w_codes[:].bitcast(FP8X4), scales=w_planes[:], in_=w_bf[:].rearrange("p i r -> p (i r)")
        )
        slope(1)

        fade_rows = sb("fade_rows", [P, T], F32, "vp1")
        for h in range(2):
            spread = bank(6 + h, "spread%d" % h)
            for c in range(PER_BANK):
                spread_column(spread[:, block(c)], FADE_ROW + PER_BANK * h + c)
            nc.scalar.copy(fade_rows[:, half(h)], spread[:])

        c0_banks = [bank(4, "c0_0"), bank(6, "c0_1")]

        def c0(k):
            return c0_banks[k // 2][:, (k % 2) * I : (k % 2 + 1) * I]

        def product(k):
            nc.tensor.matmul_mx(
                out=c0(k),
                lhsT=g_codes[0][:, block(k)].bitcast(FP8X4),
                lhsT_scale=g_planes[0][:, block(k)],
                rhs=w_codes[:].bitcast(FP8X4),
                rhs_scale=w_planes[:],
                start=True,
                stop=True,
            )

        def scaled_products():
            by_slot = bank(5, "by_slot")
            scaled = sb("scaled", [P, I // P, HALF], F32)
            for c in range(I // P):
                nc.tensor.matmul_mx(
                    out=by_slot[:, c * HALF : (c + 1) * HALF],
                    lhsT=w_codes[:, block(c)].bitcast(FP8X4),
                    lhsT_scale=w_planes[:, block(c)],
                    rhs=g_codes[1][:].bitcast(FP8X4),
                    rhs_scale=g_planes[1][:],
                    start=True,
                    stop=True,
                )
            for c in range(I // P):
                nc.scalar.activation(
                    scaled[:, c, :],
                    by_slot[:, c * HALF : (c + 1) * HALF],
                    ACT.Copy,
                    scale=cols[:, SG_ROW + c : SG_ROW + c + 1],
                )
            for k in (2, 3):
                for c in range(I // P):
                    nc.tensor.transpose(c0(k)[:, block(c)], scaled[:, c, block(k - 2)], ident[:])

        neg_gs = {}

        def slot_gradient(k, tag=None):
            neg_gs[k] = sb("neg_gs%d" % k, [P, I], F32, tag)
            if k < 2:
                nc.vector.tensor_tensor(neg_gs[k][:], c0(k), neg_slope[k][:], ALU.mult)
            else:
                nc.vector.scalar_tensor_tensor(neg_gs[k][:], vp_sq[k][:], one[:], c0(k), ALU.subtract, ALU.mult)

        def scatter(k):
            nc.vector.tensor_copy(windows[k][:].indirect(offsets[:]), neg_gs[k][:])

        def store(queue, k, h, result):
            queue.dma_start(out[block(k), half(h)], result)

        def fade_on_gpsimd(k, faded):
            for h in range(2):
                nc.gpsimd.tensor_tensor(faded[h], old_tile[k][:, half(h)], fade_rows[:, half(h)], ALU.mult)

        def finish_on_gpsimd(k, faded, halves, tag):
            result = sb("result%d" % k, [P, T], F32, tag)
            for h in halves:
                nc.gpsimd.tensor_tensor(result[:, half(h)], faded[h], windows[k][:, half(h)], ALU.subtract)
                store(nc.sync, k, h, result[:, half(h)])

        product(0)
        product(1)
        gather(2)
        gather(3)
        slot_gradient(0, "val_pool3")
        cast_grows(1)
        quantise_grows(1, "val_pool1")
        scatter(0)
        faded1_tile = sb("faded1", [P, T], F32, "g_bf1")
        faded1 = [faded1_tile[:, half(h)] for h in range(2)]
        fade_on_gpsimd(1, faded1)
        faded2 = [sb("faded2_%d" % h, [P, BANK], F32, ("neg_slope0", "vp_sq1")[h])[:] for h in range(2)]
        fade_on_gpsimd(2, faded2)
        scaled_products()
        tanh_squared(2)
        slot_gradient(1)
        slot_gradient(2)
        tanh_squared(3)
        slot_gradient(3)
        scatter(1)
        finish_on_gpsimd(1, faded1, (0, 1), "old_tile2")

        faded_t = sb("faded_t", [P, BLOCKS, 2, P], F32)
        for step, number in enumerate((7, 1, 0, 7)):
            stage = bank(number, "stage%d" % step)
            for b in range(2):
                for n in range(2):
                    nc.tensor.transpose(stage[:, block(2 * b + n)], old_pair[:, n, block(2 * step + b)], ident[:])
            for b in range(2):
                c = 2 * step + b
                nc.scalar.activation(
                    faded_t[:, c, :, :].rearrange("p n e -> p (n e)"),
                    stage[:, 2 * b * P : 2 * (b + 1) * P],
                    ACT.Copy,
                    scale=cols[:, FADE_ROW + c : FADE_ROW + c + 1],
                )

        scatter(2)
        finish_on_gpsimd(2, faded2, (0,), "g_bf1")

        for h in range(2):
            gf_stage = bank(1 - h, "gf_stage%d" % h)
            for c in range(PER_BANK):
                nc.tensor.transpose(gf_stage[:, block(c)], windows[0][:, block(PER_BANK * h + c)], ident[:])
            gf_t = sb("gf_t%d" % h, [P, BANK], F32)
            nc.scalar.activation(gf_t[:], gf_stage[:], ACT.Copy, scale=-1.0)
            total = bank(2 + h, "total%d" % h)
            for c in range(PER_BANK):
                nc.tensor.matmul(
                    total[:, block(c)],
                    faded_t[:, PER_BANK * h + c, 0, :],
                    ident[:],
                    start=c == 0,
                    stop=False,
                    is_transpose=True,
                )
            for c in range(PER_BANK):
                nc.tensor.matmul(
                    total[:, block(c)],
                    gf_t[:, block(c)],
                    ident[:],
                    start=False,
                    stop=c == PER_BANK - 1,
                    is_transpose=True,
                )
            result0 = sb("result0_%d" % h, [P, BANK], F32)
            nc.scalar.copy(result0[:], total[:])
            store(nc.sync, 0, h, result0[:])

        scatter(3)

        faded3 = [bank(1 - h, "faded3_%d" % h) for h in range(2)]
        for c in range(BLOCKS):
            nc.tensor.transpose(faded3[c // PER_BANK][:, block(c % PER_BANK)], faded_t[:, c, 1, :], ident[:])
        result3 = sb("result3", [P, T], F32, "gf_t1")
        for h in range(2):
            nc.vector.tensor_tensor(result3[:, half(h)], faded3[h][:], windows[3][:, half(h)], ALU.subtract)
            store(nc.scalar, 3, h, result3[:, half(h)])

        result2_last = sb("result2_last", [P, BANK], F32, "window0")
        nc.vector.tensor_tensor(result2_last[:], faded2[1], windows[2][:, half(1)], ALU.subtract)
        store(nc.scalar, 2, 1, result2_last[:])
